import numpy as np
import ml_dtypes


def mxq(x, axis, fmt="e4m3"):
    dtype, down = {"e4m3": (ml_dtypes.float8_e4m3fn, 7), "e5m2": (ml_dtypes.float8_e5m2, 14)}[fmt]
    v = np.moveaxis(np.asarray(x, np.float32).astype(ml_dtypes.bfloat16).astype(np.float64), axis, -1)
    blocks = v.reshape(v.shape[:-1] + (-1, 32))
    amax = np.abs(blocks).max(-1, keepdims=True)
    byte = np.maximum(np.where(amax > 0, np.frexp(amax)[1] - 1 + 127, 0) - down, 1)
    scale = np.exp2(byte - 127.0)
    codes = (blocks / scale).astype(np.float32).astype(dtype).astype(np.float64)
    return np.moveaxis((codes * scale).reshape(v.shape), -1, axis)


WIDE = False


def mx_kscale(k):
    if not WIDE:
        return np.ones(k)
    levels = np.array([10, -10, 5, -5, 0])
    if k % 512:
        return np.exp2(np.random.permutation(np.resize(levels, k // 32))).repeat(32)
    a = np.empty((k // 512, 16))
    for p in range(k // 512):
        a[p, :8] = np.random.permutation(np.resize(levels, 8))
        for g in range(8):
            far = levels[np.abs(levels - a[p, g]) >= 10]
            a[p, g + 8] = far[np.random.randint(len(far))]
    return np.exp2(a.ravel()).repeat(32)


def f64(x):
    return np.asarray(x).astype(np.float64)


def striped(idx):
    return np.tile(idx.reshape(-1, 16).T, (8, 1)).astype(np.uint16)


def unstriped(offs):
    return offs[:16].T.reshape(-1).astype(np.int64)


def striped8(idx):
    return np.concatenate([x.reshape(-1, 16).T for x in idx]).astype(np.uint16)


def runs(offs, k):
    lists = np.stack([offs[16 * r : 16 * r + 16].T.reshape(-1) for r in range(8)]).astype(np.int64)
    return lists[np.arange(k) % 512 // 64]


def pack_weight(w):
    k, n = w.shape
    w = f64(np.asarray(w, np.float32).astype(ml_dtypes.bfloat16)).reshape(k // 32, 32, n)
    amax = np.abs(w).max(1)
    byte = np.clip(np.where(amax > 0, np.frexp(amax)[1] - 1 + 127 - 7, 1), 1, 254)
    scaled = (w * np.exp2(127.0 - byte)[:, None, :]).reshape(k, n).astype(np.float32)
    words = np.ascontiguousarray(scaled.reshape(k // 512, 128, 4, n).transpose(0, 1, 3, 2)).astype(ml_dtypes.float8_e4m3fn).view(np.uint8)
    return words, np.ascontiguousarray(byte.astype(np.uint8).reshape(k // 512, 16, n))


def unpack_weight(words, scales):
    g, p, n, _ = words.shape
    vals = np.ascontiguousarray(words).view(ml_dtypes.float8_e4m3fn).astype(np.float64) * np.repeat(np.exp2(scales.astype(np.float64) - 127.0), 8, axis=1)[..., None]
    return vals.transpose(0, 1, 3, 2).reshape(g * 512, n)


E2M1 = np.array([0.0, 0.5, 1.0, 1.5, 2.0, 3.0, 4.0, 6.0, -0.0, -0.5, -1.0, -1.5, -2.0, -3.0, -4.0, -6.0])


def pack_fp4(w):
    k, n = w.shape
    w = f64(np.asarray(w, np.float32).astype(ml_dtypes.bfloat16)).reshape(k // 32, 32, n)
    amax = np.abs(w).max(1)
    mant, ex = np.frexp(amax / 6.0)
    byte = np.clip(np.where(amax > 0, np.where(mant > 0.5, ex, ex - 1) + 127, 1), 1, 254)
    scaled = (w * np.exp2(127.0 - byte)[:, None, :]).reshape(k, n).astype(np.float32)
    c = np.ascontiguousarray(scaled.reshape(k // 512, 128, 4, n).transpose(0, 1, 3, 2)).astype(ml_dtypes.float4_e2m1fn).view(np.uint8) & 0xF
    words = (c[..., 0::2] | (c[..., 1::2] << 4)).reshape(k // 512, 128, 2 * n)
    return np.ascontiguousarray(words), np.ascontiguousarray(byte.astype(np.uint8).reshape(k // 512, 16, n))


def unpack_fp4(words, scales):
    g, _, n = scales.shape
    words = np.ascontiguousarray(words).reshape(g, 128, n, 2)
    nib = np.empty((g, 128, n, 4), np.uint8)
    nib[..., 0::2] = words & 0xF
    nib[..., 1::2] = words >> 4
    vals = E2M1[nib] * np.repeat(np.exp2(scales.astype(np.float64) - 127.0), 8, axis=1)[..., None]
    return vals.transpose(0, 1, 3, 2).reshape(g * 512, n)


def planes(y):
    n, m = y.shape
    v = y.astype(np.float32).astype(ml_dtypes.bfloat16).astype(np.float64).reshape(n // 32, 32, m)
    top = np.abs(v).max(1)
    byte = np.clip(np.where(top > 0, np.frexp(top)[1] - 1 + 127 - 7, 1), 1, 254)
    codes = (v * np.exp2(127.0 - byte)[:, None, :]).reshape(n, m).astype(np.float32).astype(ml_dtypes.float8_e4m3fn).view(np.uint8)
    words = codes.reshape(n // 512, 128, 4, m).transpose(0, 1, 3, 2)
    return np.ascontiguousarray(words), np.ascontiguousarray(byte.astype(np.uint8).reshape(n // 512, 16, m))


K, T, S, V, H = 512, 2048, 512, 512, 512


def setup_inputs():
    n = np.random.standard_normal
    s = mx_kscale(K)[:, None]
    u = mx_kscale(S)
    packed_xT = pack_weight(n((K, T)) * s)
    packed_w1 = pack_fp4(n((K, H)) / np.sqrt(K) / s)
    packed_w2 = pack_fp4(n((K, H)) / np.sqrt(K) / s)
    return {
        "x_words": packed_xT[0],
        "x_scales": packed_xT[1],
        "w1_words": packed_w1[0],
        "w1_scales": packed_w1[1],
        "w2_words": packed_w2[0],
        "w2_scales": packed_w2[1],
        "ga": (np.random.uniform(0.5, 1.5, (H, 1)) * u[:, None]).astype(np.float32),
        "gb": (np.random.uniform(0.5, 1.5, (H, 1)) / u[:, None]).astype(np.float32),
        "offs": striped(np.random.permutation(T)[:S]),
        "two": striped(np.random.permutation(T)[:V]),
        "n1": striped8(np.stack([np.random.permutation(S) for _ in range(8)])),
        "n2": striped8(np.stack([np.random.permutation(S) for _ in range(8)])),
        "n3": striped8(np.stack([np.random.permutation(V) for _ in range(8)])),
        "n4": striped8(np.stack([np.random.permutation(V) for _ in range(8)])),
        "n5": striped8(np.stack([np.random.permutation(V) for _ in range(8)])),
        "n6": striped8(np.stack([np.random.permutation(V) for _ in range(8)])),
    }


def reference(x_words, x_scales, w1_words, w1_scales, w2_words, w2_scales, ga, gb, offs, two, n1, n2, n3, n4, n5, n6):
    xq = unpack_weight(x_words, x_scales)[:, unstriped(offs)]
    a = unpack_fp4(w1_words, w1_scales).T @ xq
    z = f64(ga) * (a * (a[np.arange(H)[:, None], runs(n1, H)] - (a[np.arange(H)[:, None], runs(n2, H)])))
    x_two = unpack_weight(x_words, x_scales)[:, unstriped(two)]
    b = unpack_fp4(w2_words, w2_scales).T @ x_two
    z2 = f64(gb) * ((b * (b[np.arange(H)[:, None], runs(n3, H)])) * (np.tanh(b[np.arange(H)[:, None], runs(n4, H)])))
    s = 0.0625 * ((mxq(z, 0, "e4m3").T @ mxq(z2, 0, "e4m3")))
    ex = np.exp(0.5 * s)
    out_0 = (2.0 * ex) / (ex + ex[np.arange(S)[:, None], runs(n5, S)] + ex[np.arange(S)[:, None], runs(n6, S)])
    return (out_0,) + planes(out_0)

@@ -1,0 +1,262 @@
+from contextlib import ExitStack
+
+import concourse.mybir as mybir
+from concourse.masks import make_identity
+
+FLOPS = 805306368
+
+F32 = mybir.dt.float32
+BF16 = mybir.dt.bfloat16
+I32 = mybir.dt.int32
+U32 = mybir.dt.uint32
+U16 = mybir.dt.uint16
+U8 = mybir.dt.uint8
+FP8X4 = mybir.dt.float8_e4m3fn_x4
+FP4X4 = mybir.dt.float4_e2m1fn_x4
+ACT = mybir.ActivationFunctionType
+ALU = mybir.AluOpType
+
+P = 128
+T = 2048
+S = 512
+PLANES = 4
+HALVES = [(0, 256), (256, 512)]
+TAIL = [(0, 256), (256, 384), (384, 512)]
+
+
+def tile_picked_kqwindcubeshare_none_po_kernel(
+    tc, x_words, x_scales, w1_words, w1_scales, w2_words, w2_scales, ga, gb,
+    offs, two, n1, n2, n3, n4, n5, n6, out_0, out_1, out_2,
+):
+    nc = tc.nc
+    with ExitStack() as ctx:
+        keep = ctx.enter_context(tc.tile_pool(name="keep", bufs=1))
+        psum = ctx.enter_context(tc.psum_pool(name="psum", bufs=1))
+
+        def sb(name, shape, dtype):
+            return keep.tile(shape, dtype, name=name, align_bytes=64)
+
+        def load_list(name, src):
+            t = keep.tile([P, S // 16], U16, name=name)
+            nc.sync.dma_start(t[:], src)
+            return t
+
+        def load_scale_rows(dst, src, queue):
+            for q in range(4):
+                queue.dma_start(dst[32 * q : 32 * q + 4, :].bitcast(I32), src[0, 4 * q : 4 * q + 4, :].bitcast(I32))
+
+        def entries(lst, c0, c1):
+            return lst[:, c0 // 16 : c1 // 16]
+
+        xs = sb("xs", [P, T], U8)
+        xw = sb("xw", [P, T], U32)
+        w1s_raw = sb("w1s_raw", [P, S], U8)
+        w2s_raw = sb("w2s_raw", [P, S], U8)
+        w1w_raw = sb("w1w_raw", [P, 2 * S], U8)
+        w2w_raw = sb("w2w_raw", [P, 2 * S], U8)
+        g_rows = sb("g_rows", [P, P], F32)
+        ident = sb("ident", [P, P], F32)
+        warm = sb("warm", [P, 2], F32)
+
+        nc.gpsimd.memset(xs[:].bitcast(I32), 0)
+        nc.vector.memset(w1s_raw[:].bitcast(I32), 0)
+        nc.vector.memset(w2s_raw[:].bitcast(I32), 0)
+        nc.gpsimd.memset(g_rows[:], 0.0)
+        for i, g in enumerate((ga, gb)):
+            nc.gpsimd.dma_start(
+                g_rows[4 * i : 4 * i + 4, :].rearrange("t (g q) -> t g q", q=8),
+                g.rearrange("(g t q) o -> t g (q o)", t=4, q=8),
+            )
+        make_identity(nc, ident[:])
+        nc.vector.memset(warm[:, 0:1], 0.0)
+        nc.scalar.activation(warm[:, 1:2], warm[:, 0:1], ACT.Sigmoid)
+
+        l_offs = load_list("l_offs", offs)
+        l_two = load_list("l_two", two)
+        nc.sync.dma_start(w1w_raw[:].bitcast(I32), w1_words[0].bitcast(I32))
+        load_scale_rows(xs, x_scales, nc.sync)
+        nc.sync.dma_start(xw[:].bitcast(I32), x_words[0].rearrange("p n t -> p (n t)").bitcast(I32))
+        load_scale_rows(w1s_raw, w1_scales, nc.sync)
+        l_n2 = load_list("l_n2", n2)
+        l_n1 = load_list("l_n1", n1)
+        nc.sync.dma_start(w2w_raw[:].bitcast(I32), w2_words[0].bitcast(I32))
+        load_scale_rows(w2s_raw, w2_scales, nc.sync)
+        l_n4 = load_list("l_n4", n4)
+        l_n3 = load_list("l_n3", n3)
+        l_n5 = load_list("l_n5", n5)
+        l_n6 = load_list("l_n6", n6)
+
+        def deal(name, raw_words, raw_scales):
+            words = sb(name + "_words", [P, 2 * S], U8)
+            scales = sb(name + "_scales", [P, S], U8)
+            for dst, src, w in ((words, raw_words, 4), (scales, raw_scales, 2)):
+                nc.vector.tensor_copy(
+                    dst[:].bitcast(I32).rearrange("p (t g w) -> p t g w", t=4, w=w),
+                    src[:].bitcast(I32).rearrange("p (g t w) -> p t g w", t=4, w=w),
+                )
+            return words, scales
+
+        xa_s = sb("xa_s", [P, S], U8)
+        xb_s = sb("xb_s", [P, S], U8)
+        xa_w = sb("xa_w", [P, S], U32)
+        xb_w = sb("xb_w", [P, S], U32)
+        nc.vector.tensor_copy(xa_s[:], xs[:].indirect(l_offs[:]))
+        nc.vector.tensor_copy(xb_s[:], xs[:].indirect(l_two[:]))
+        w1w, w1s = deal("w1", w1w_raw, w1s_raw)
+        nc.vector.tensor_copy(xa_w[:], xw[:].indirect(l_offs[:]))
+        nc.vector.tensor_copy(xb_w[:], xw[:].indirect(l_two[:]))
+        w2w, w2s = deal("w2", w2w_raw, w2s_raw)
+
+        g_bank = psum.tile([P, P], F32, name="g_bank", tag="bankB3")
+        nc.tensor.transpose(g_bank[:], g_rows[:], ident[:])
+        g_cols = sb("g_cols", [P, 8], F32)
+        nc.scalar.copy(g_cols[:], g_bank[:, 0:8])
+
+        def project(name, tag, ww, ws, xwords, xscales):
+            banks, windows = [], []
+            for t in range(PLANES):
+                bank = psum.tile([P, S], F32, name=name + "_bank%d" % t, tag=tag + "%d" % t)
+                nc.tensor.matmul_mx(
+                    bank[:],
+                    lhsT=ww[:, 256 * t : 256 * (t + 1)].bitcast(FP4X4),
+                    lhsT_scale=ws[:, P * t : P * (t + 1)],
+                    rhs=xwords[:].bitcast(FP8X4),
+                    rhs_scale=xscales[:],
+                    start=True,
+                    stop=True,
+                )
+                win = sb(name + "_win%d" % t, [P, S], F32)
+                nc.scalar.copy(win[:], bank[:])
+                banks.append(bank)
+                windows.append(win)
+            return banks, windows
+
+        a_banks, a_win = project("a", "bankA", w1w, w1s, xa_w, xa_s)
+        b_banks, b_win = project("b", "bankB", w2w, w2s, xb_w, xb_s)
+
+        ga_a = sb("ga_a", [P, PLANES, S], F32)
+        gb_b = sb("gb_b", [P, PLANES, S], F32)
+        for t in range(PLANES):
+            nc.scalar.activation(ga_a[:, t, :], a_banks[t][:], ACT.Copy, scale=g_cols[:, t : t + 1])
+        for t in range(PLANES):
+            nc.scalar.activation(gb_b[:, t, :], b_banks[t][:], ACT.Copy, scale=g_cols[:, 4 + t : 5 + t])
+
+        tanh4 = []
+        for c, (c0, c1) in enumerate(HALVES):
+            sig = sb("sig%d" % c, [P, PLANES, c1 - c0], F32)
+            th = sb("tanh%d" % c, [P, PLANES, c1 - c0], F32)
+            for t in range(PLANES):
+                nc.scalar.activation(sig[:, t, :], b_win[t][:].indirect(entries(l_n4, c0, c1)), ACT.Sigmoid, scale=2.0)
+            nc.scalar.activation(th[:], sig[:], ACT.Copy, scale=2.0, bias=-1.0)
+            tanh4.append(th)
+
+        zb = sb("zb", [P, PLANES * S], BF16)
+        zb_view = zb[:].rearrange("p (u m t) -> p m t u", u=4, t=4)
+        ga_a_view = ga_a[:].rearrange("p t (m u) -> p m t u", u=4)
+        diffs = []
+        for c, (c0, c1) in enumerate(HALVES):
+            second = sb("second%d" % c, [P, PLANES, c1 - c0], F32)
+            diff = sb("diff%d" % c, [P, PLANES, c1 - c0], F32)
+            for t in range(PLANES):
+                nc.vector.tensor_copy(second[:, t, :], a_win[t][:].indirect(entries(l_n2, c0, c1)))
+            for t in range(PLANES):
+                nc.vector.tensor_tensor(diff[:, t, :], a_win[t][:].indirect(entries(l_n1, c0, c1)), second[:, t, :], ALU.subtract)
+            diffs.append(diff)
+        for c, (c0, c1) in enumerate(HALVES):
+            nc.vector.tensor_tensor(
+                zb_view[:, c0 // 4 : c1 // 4],
+                diffs[c][:].rearrange("p t (m u) -> p m t u", u=4),
+                ga_a_view[:, c0 // 4 : c1 // 4],
+                ALU.mult,
+            )
+
+        third = []
+        for c, (c0, c1) in enumerate(HALVES):
+            prod = sb("third%d" % c, [P, PLANES, c1 - c0], F32)
+            for t in range(PLANES):
+                nc.vector.tensor_tensor(prod[:, t, :], b_win[t][:].indirect(entries(l_n3, c0, c1)), gb_b[:, t, c0:c1], ALU.mult)
+            third.append(prod)
+            if c == 0:
+                zw = sb("zw", [P, S], U32)
+                zs = sb("zs", [P, S], U8)
+                nc.vector.quantize_mx(zw[:].bitcast(FP8X4), zs[:], zb[:])
+
+        s_banks = [psum.tile([P, S], F32, name="s_bank%d" % t, tag="bankA%d" % t) for t in range(PLANES)]
+        ex_win = [sb("ex_win%d" % t, [P, S], F32) for t in range(PLANES)]
+        ex4 = sb("ex4", [P, PLANES, S], F32)
+        z2b = []
+        for c, (c0, c1) in enumerate(HALVES):
+            zc = sb("z2b%d" % c, [P, PLANES * (c1 - c0)], BF16)
+            nc.vector.tensor_tensor(
+                zc[:].rearrange("p (c i t) -> p c t i", i=4, t=4),
+                third[c][:].rearrange("p t (c i) -> p c t i", i=4),
+                tanh4[c][:].rearrange("p t (c i) -> p c t i", i=4),
+                ALU.mult,
+            )
+            z2b.append(zc)
+        for c, (c0, c1) in enumerate(HALVES):
+            z2w = sb("z2w%d" % c, [P, c1 - c0], U32)
+            z2s = sb("z2s%d" % c, [P, c1 - c0], U8)
+            nc.vector.quantize_mx(z2w[:].bitcast(FP8X4), z2s[:], z2b[c][:])
+            for t in range(PLANES):
+                nc.tensor.matmul_mx(
+                    s_banks[t][:, c0:c1],
+                    lhsT=zw[:, P * t : P * (t + 1)].bitcast(FP8X4),
+                    lhsT_scale=zs[:, P * t : P * (t + 1)],
+                    rhs=z2w[:].bitcast(FP8X4),
+                    rhs_scale=z2s[:],
+                    start=True,
+                    stop=True,
+                )
+            for t in range(PLANES):
+                nc.scalar.activation(ex_win[t][:, c0:c1], s_banks[t][:, c0:c1], ACT.Exp, scale=0.03125)
+                nc.scalar.activation(ex4[:, t, c0:c1], s_banks[t][:, c0:c1], ACT.Exp, scale=0.03125)
+
+        yw = sb("yw", [P, S], U32)
+        ys = sb("ys", [P, S], U8)
+        out_rows = out_0.rearrange("(p t) v -> p t v", t=4)
+        out_words = out_1[0].rearrange("p n t -> p (n t)").bitcast(I32)
+
+        def gathers(c):
+            c0, c1 = TAIL[c]
+            part = sb("part%d" % c, [P, PLANES, c1 - c0], F32)
+            den = sb("den%d" % c, [P, PLANES, c1 - c0], F32)
+            for t in range(PLANES):
+                nc.vector.tensor_tensor(part[:, t, :], ex_win[t][:].indirect(entries(l_n5, c0, c1)), ex4[:, t, c0:c1], ALU.add)
+            for t in range(PLANES):
+                nc.vector.tensor_tensor(den[:, t, :], ex_win[t][:].indirect(entries(l_n6, c0, c1)), part[:, t, :], ALU.add)
+            root = sb("root%d" % c, [P, PLANES, c1 - c0], F32)
+            inv = sb("inv%d" % c, [P, PLANES, c1 - c0], F32)
+            nc.scalar.activation(root[:], den[:], ACT.Abs_reciprocal_sqrt, scale=0.5)
+            nc.scalar.activation(inv[:], root[:], ACT.Square)
+            return inv
+
+        def finish(c, inv):
+            c0, c1 = TAIL[c]
+            y = sb("y%d" % c, [P, PLANES, c1 - c0], F32)
+            nc.vector.tensor_tensor(y[:], ex4[:, :, c0:c1], inv[:], ALU.mult)
+            nc.sync.dma_start(out_rows[:, :, c0:c1], y[:])
+            yb = sb("yb%d" % c, [P, PLANES * (c1 - c0)], BF16)
+            nc.scalar.copy(
+                yb[:].rearrange("p (c i t) -> p c t i", i=4, t=4),
+                y[:].rearrange("p t (c i) -> p c t i", i=4),
+            )
+            return yb
+
+        def planes(c, yb):
+            c0, c1 = TAIL[c]
+            nc.vector.quantize_mx(yw[:, c0:c1].bitcast(FP8X4), ys[:, c0:c1], yb[:])
+            nc.sync.dma_start(out_words[:, c0:c1], yw[:, c0:c1].bitcast(I32))
+
+        inv0 = gathers(0)
+        inv1 = gathers(1)
+        yb0 = finish(0, inv0)
+        inv2 = gathers(2)
+        yb1 = finish(1, inv1)
+        planes(0, yb0)
+        yb2 = finish(2, inv2)
+        planes(1, yb1)
+        planes(2, yb2)
+        for q in range(4):
+            queue = nc.scalar if q % 2 else nc.sync
+            queue.dma_start(out_2[0, 4 * q : 4 * q + 4, :].bitcast(I32), ys[32 * q : 32 * q + 4, :].bitcast(I32))

@@ -33,8 +33,8 @@ def tile_picked_kqwindcubeshare_none_po_kernel(
         keep = ctx.enter_context(tc.tile_pool(name="keep", bufs=1))
         psum = ctx.enter_context(tc.psum_pool(name="psum", bufs=1))
 
-        def sb(name, shape, dtype):
-            return keep.tile(shape, dtype, name=name, align_bytes=64)
+        def sb(name, shape, dtype, tag=None):
+            return keep.tile(shape, dtype, name=name, tag=tag or name, align_bytes=64)
 
         def load_list(name, src):
             t = keep.tile([P, S // 16], U16, name=name)
@@ -90,7 +90,7 @@ def tile_picked_kqwindcubeshare_none_po_kernel(
             words = sb(name + "_words", [P, 2 * S], U8)
             scales = sb(name + "_scales", [P, S], U8)
             for dst, src, w in ((words, raw_words, 4), (scales, raw_scales, 2)):
-                nc.vector.tensor_copy(
+                nc.gpsimd.tensor_copy(
                     dst[:].bitcast(I32).rearrange("p (t g w) -> p t g w", t=4, w=w),
                     src[:].bitcast(I32).rearrange("p (g t w) -> p t g w", t=4, w=w),
                 )
@@ -150,54 +150,11 @@ def tile_picked_kqwindcubeshare_none_po_kernel(
             nc.scalar.activation(th[:], sig[:], ACT.Copy, scale=2.0, bias=-1.0)
             tanh4.append(th)
 
-        zb = sb("zb", [P, PLANES * S], BF16)
-        zb_view = zb[:].rearrange("p (u m t) -> p m t u", u=4, t=4)
-        ga_a_view = ga_a[:].rearrange("p t (m u) -> p m t u", u=4)
-        diffs = []
-        for c, (c0, c1) in enumerate(HALVES):
-            second = sb("second%d" % c, [P, PLANES, c1 - c0], F32)
-            diff = sb("diff%d" % c, [P, PLANES, c1 - c0], F32)
-            for t in range(PLANES):
-                nc.vector.tensor_copy(second[:, t, :], a_win[t][:].indirect(entries(l_n2, c0, c1)))
-            for t in range(PLANES):
-                nc.vector.tensor_tensor(diff[:, t, :], a_win[t][:].indirect(entries(l_n1, c0, c1)), second[:, t, :], ALU.subtract)
-            diffs.append(diff)
-        for c, (c0, c1) in enumerate(HALVES):
-            nc.vector.tensor_tensor(
-                zb_view[:, c0 // 4 : c1 // 4],
-                diffs[c][:].rearrange("p t (m u) -> p m t u", u=4),
-                ga_a_view[:, c0 // 4 : c1 // 4],
-                ALU.mult,
-            )
-
-        third = []
-        for c, (c0, c1) in enumerate(HALVES):
-            prod = sb("third%d" % c, [P, PLANES, c1 - c0], F32)
-            for t in range(PLANES):
-                nc.vector.tensor_tensor(prod[:, t, :], b_win[t][:].indirect(entries(l_n3, c0, c1)), gb_b[:, t, c0:c1], ALU.mult)
-            third.append(prod)
-            if c == 0:
-                zw = sb("zw", [P, S], U32)
-                zs = sb("zs", [P, S], U8)
-                nc.vector.quantize_mx(zw[:].bitcast(FP8X4), zs[:], zb[:])
-
-        s_banks = [psum.tile([P, S], F32, name="s_bank%d" % t, tag="bankA%d" % t) for t in range(PLANES)]
-        ex_win = [sb("ex_win%d" % t, [P, S], F32) for t in range(PLANES)]
-        ex4 = sb("ex4", [P, PLANES, S], F32)
-        z2b = []
-        for c, (c0, c1) in enumerate(HALVES):
-            zc = sb("z2b%d" % c, [P, PLANES * (c1 - c0)], BF16)
-            nc.vector.tensor_tensor(
-                zc[:].rearrange("p (c i t) -> p c t i", i=4, t=4),
-                third[c][:].rearrange("p t (c i) -> p c t i", i=4),
-                tanh4[c][:].rearrange("p t (c i) -> p c t i", i=4),
-                ALU.mult,
-            )
-            z2b.append(zc)
-        for c, (c0, c1) in enumerate(HALVES):
+        def scores(c, zc):
+            c0, c1 = HALVES[c]
             z2w = sb("z2w%d" % c, [P, c1 - c0], U32)
             z2s = sb("z2s%d" % c, [P, c1 - c0], U8)
-            nc.vector.quantize_mx(z2w[:].bitcast(FP8X4), z2s[:], z2b[c][:])
+            nc.vector.quantize_mx(z2w[:].bitcast(FP8X4), z2s[:], zc[:])
             for t in range(PLANES):
                 nc.tensor.matmul_mx(
                     s_banks[t][:, c0:c1],
@@ -210,7 +167,48 @@ def tile_picked_kqwindcubeshare_none_po_kernel(
                 )
             for t in range(PLANES):
                 nc.scalar.activation(ex_win[t][:, c0:c1], s_banks[t][:, c0:c1], ACT.Exp, scale=0.03125)
+            for t in range(PLANES):
                 nc.scalar.activation(ex4[:, t, c0:c1], s_banks[t][:, c0:c1], ACT.Exp, scale=0.03125)
+
+        zb = sb("zb", [P, PLANES * S], BF16)
+        zb_view = zb[:].rearrange("p (u m t) -> p m t u", u=4, t=4)
+        ga_a_view = ga_a[:].rearrange("p t (m u) -> p m t u", u=4)
+        seconds = [sb("second%d" % c, [P, PLANES, c1 - c0], F32) for c, (c0, c1) in enumerate(HALVES)]
+        diffs = [sb("diff%d" % c, [P, PLANES, c1 - c0], F32) for c, (c0, c1) in enumerate(HALVES)]
+        for t in range(PLANES):
+            for c, (c0, c1) in enumerate(HALVES):
+                nc.vector.tensor_copy(seconds[c][:, t, :], a_win[t][:].indirect(entries(l_n2, c0, c1)))
+            for c, (c0, c1) in enumerate(HALVES):
+                nc.vector.tensor_tensor(diffs[c][:, t, :], a_win[t][:].indirect(entries(l_n1, c0, c1)), seconds[c][:, t, :], ALU.subtract)
+        for c, (c0, c1) in enumerate(HALVES):
+            nc.vector.tensor_tensor(
+                zb_view[:, c0 // 4 : c1 // 4],
+                diffs[c][:].rearrange("p t (m u) -> p m t u", u=4),
+                ga_a_view[:, c0 // 4 : c1 // 4],
+                ALU.mult,
+            )
+
+        s_banks = [psum.tile([P, S], F32, name="s_bank%d" % t, tag="bankA%d" % t) for t in range(PLANES)]
+        ex_win = [sb("ex_win%d" % t, [P, S], F32) for t in range(PLANES)]
+        ex4 = sb("ex4", [P, PLANES, S], F32)
+        zw = sb("zw", [P, S], U32)
+        zs = sb("zs", [P, S], U8)
+        for c, (c0, c1) in enumerate(HALVES):
+            prod = sb("third%d" % c, [P, PLANES, c1 - c0], F32, tag="tanh0" if c == 1 else None)
+            for t in range(PLANES):
+                nc.vector.tensor_tensor(prod[:, t, :], b_win[t][:].indirect(entries(l_n3, c0, c1)), gb_b[:, t, c0:c1], ALU.mult)
+                if c == 0 and t == 0:
+                    nc.vector.quantize_mx(zw[:].bitcast(FP8X4), zs[:], zb[:])
+                if c == 1 and t == 0:
+                    scores(0, zc)
+            zc = sb("z2b%d" % c, [P, PLANES * (c1 - c0)], BF16)
+            nc.vector.tensor_tensor(
+                zc[:].rearrange("p (c i t) -> p c t i", i=4, t=4),
+                prod[:].rearrange("p t (c i) -> p c t i", i=4),
+                tanh4[c][:].rearrange("p t (c i) -> p c t i", i=4),
+                ALU.mult,
+            )
+        scores(1, zc)
 
         yw = sb("yw", [P, S], U32)
         ys = sb("ys", [P, S], U8)
@@ -219,7 +217,7 @@ def tile_picked_kqwindcubeshare_none_po_kernel(
 
         def gathers(c):
             c0, c1 = TAIL[c]
-            part = sb("part%d" % c, [P, PLANES, c1 - c0], F32)
+            part = sb("part%d" % c, [P, PLANES, c1 - c0], F32, tag="inv0" if c == 2 else None)
             den = sb("den%d" % c, [P, PLANES, c1 - c0], F32)
             for t in range(PLANES):
                 nc.vector.tensor_tensor(part[:, t, :], ex_win[t][:].indirect(entries(l_n5, c0, c1)), ex4[:, t, c0:c1], ALU.add)
@@ -227,8 +225,9 @@ def tile_picked_kqwindcubeshare_none_po_kernel(
                 nc.vector.tensor_tensor(den[:, t, :], ex_win[t][:].indirect(entries(l_n6, c0, c1)), part[:, t, :], ALU.add)
             root = sb("root%d" % c, [P, PLANES, c1 - c0], F32)
             inv = sb("inv%d" % c, [P, PLANES, c1 - c0], F32)
-            nc.scalar.activation(root[:], den[:], ACT.Abs_reciprocal_sqrt, scale=0.5)
-            nc.scalar.activation(inv[:], root[:], ACT.Square)
+            for t0, t1 in ((0, 2), (2, 4)) if c == 2 else ((0, 4),):
+                nc.scalar.activation(root[:, t0:t1, :], den[:, t0:t1, :], ACT.Abs_reciprocal_sqrt, scale=0.5)
+                nc.scalar.activation(inv[:, t0:t1, :], root[:, t0:t1, :], ACT.Square)
             return inv
 
         def finish(c, inv):
@@ -237,7 +236,8 @@ def tile_picked_kqwindcubeshare_none_po_kernel(
             nc.vector.tensor_tensor(y[:], ex4[:, :, c0:c1], inv[:], ALU.mult)
             nc.sync.dma_start(out_rows[:, :, c0:c1], y[:])
             yb = sb("yb%d" % c, [P, PLANES * (c1 - c0)], BF16)
-            nc.scalar.copy(
+            move = nc.vector.tensor_copy if c == 2 else nc.scalar.copy
+            move(
                 yb[:].rearrange("p (c i t) -> p c t i", i=4, t=4),
                 y[:].rearrange("p t (c i) -> p c t i", i=4),
             )

@@ -21,7 +21,6 @@ T = 2048
 S = 512
 PLANES = 4
 HALVES = [(0, 256), (256, 512)]
-TAIL = [(0, 256), (256, 384), (384, 512)]
 
 
 def tile_picked_kqwindcubeshare_none_po_kernel(
@@ -62,14 +61,12 @@ def tile_picked_kqwindcubeshare_none_po_kernel(
         nc.vector.memset(w1s_raw[:].bitcast(I32), 0)
         nc.vector.memset(w2s_raw[:].bitcast(I32), 0)
         nc.gpsimd.memset(g_rows[:], 0.0)
-        for i, g in enumerate((ga, gb)):
-            nc.gpsimd.dma_start(
-                g_rows[4 * i : 4 * i + 4, :].rearrange("t (g q) -> t g q", q=8),
-                g.rearrange("(g t q) o -> t g (q o)", t=4, q=8),
-            )
         make_identity(nc, ident[:])
         nc.vector.memset(warm[:, 0:1], 0.0)
         nc.scalar.activation(warm[:, 1:2], warm[:, 0:1], ACT.Sigmoid)
+
+        a_win = [sb("a_win%d" % t, [P, 2 * S], F32) for t in range(PLANES)]
+        b_win = [sb("b_win%d" % t, [P, 2 * S], F32) for t in range(PLANES)]
 
         l_offs = load_list("l_offs", offs)
         l_two = load_list("l_two", two)
@@ -81,6 +78,11 @@ def tile_picked_kqwindcubeshare_none_po_kernel(
         l_n1 = load_list("l_n1", n1)
         nc.sync.dma_start(w2w_raw[:].bitcast(I32), w2_words[0].bitcast(I32))
         load_scale_rows(w2s_raw, w2_scales, nc.sync)
+        for i, g in enumerate((ga, gb)):
+            nc.sync.dma_start(
+                g_rows[4 * i : 4 * i + 4, :].rearrange("t (g q) -> t g q", q=8),
+                g.rearrange("(g t q) o -> t g (q o)", t=4, q=8),
+            )
         l_n4 = load_list("l_n4", n4)
         l_n3 = load_list("l_n3", n3)
         l_n5 = load_list("l_n5", n5)
@@ -109,11 +111,13 @@ def tile_picked_kqwindcubeshare_none_po_kernel(
 
         g_bank = psum.tile([P, P], F32, name="g_bank", tag="bankB3")
         nc.tensor.transpose(g_bank[:], g_rows[:], ident[:])
-        g_cols = sb("g_cols", [P, 8], F32)
-        nc.scalar.copy(g_cols[:], g_bank[:, 0:8])
+        g_cols = sb("g_cols", [P, 12], F32)
+        nc.scalar.copy(g_cols[:, 0:4], g_bank[:, 0:4])
+        nc.scalar.activation(g_cols[:, 4:8], g_bank[:, 4:8], ACT.Copy, scale=2.0)
+        nc.scalar.activation(g_cols[:, 8:12], g_bank[:, 4:8], ACT.Copy, scale=-1.0)
 
-        def project(name, tag, ww, ws, xwords, xscales):
-            banks, windows = [], []
+        def project(name, tag, ww, ws, xwords, xscales, windows):
+            banks = []
             for t in range(PLANES):
                 bank = psum.tile([P, S], F32, name=name + "_bank%d" % t, tag=tag + "%d" % t)
                 nc.tensor.matmul_mx(
@@ -125,138 +129,142 @@ def tile_picked_kqwindcubeshare_none_po_kernel(
                     start=True,
                     stop=True,
                 )
-                win = sb(name + "_win%d" % t, [P, S], F32)
-                nc.scalar.copy(win[:], bank[:])
+                nc.scalar.copy(windows[t][:, 0:S], bank[:])
                 banks.append(bank)
-                windows.append(win)
-            return banks, windows
+            return banks
 
-        a_banks, a_win = project("a", "bankA", w1w, w1s, xa_w, xa_s)
-        b_banks, b_win = project("b", "bankB", w2w, w2s, xb_w, xb_s)
+        a_banks = project("a", "bankA", w1w, w1s, xa_w, xa_s, a_win)
+        project("b", "bankB", w2w, w2s, xb_w, xb_s, b_win)
 
         ga_a = sb("ga_a", [P, PLANES, S], F32)
-        gb_b = sb("gb_b", [P, PLANES, S], F32)
+        b_plain = sb("b_plain", [P, PLANES, S], F32)
+        for t in range(PLANES):
+            nc.sync.dma_start(b_plain[:, t, :], b_win[t][:, 0:S])
         for t in range(PLANES):
             nc.scalar.activation(ga_a[:, t, :], a_banks[t][:], ACT.Copy, scale=g_cols[:, t : t + 1])
+
+        sig = sb("sig", [P, PLANES, S], F32)
+        gb_tanh = sb("gb_tanh", [P, PLANES, S], F32)
         for t in range(PLANES):
-            nc.scalar.activation(gb_b[:, t, :], b_banks[t][:], ACT.Copy, scale=g_cols[:, 4 + t : 5 + t])
-
-        tanh4 = []
-        for c, (c0, c1) in enumerate(HALVES):
-            sig = sb("sig%d" % c, [P, PLANES, c1 - c0], F32)
-            th = sb("tanh%d" % c, [P, PLANES, c1 - c0], F32)
-            for t in range(PLANES):
-                nc.scalar.activation(sig[:, t, :], b_win[t][:].indirect(entries(l_n4, c0, c1)), ACT.Sigmoid, scale=2.0)
-            nc.scalar.activation(th[:], sig[:], ACT.Copy, scale=2.0, bias=-1.0)
-            tanh4.append(th)
-
-        def scores(c, zc):
-            c0, c1 = HALVES[c]
-            z2w = sb("z2w%d" % c, [P, c1 - c0], U32)
-            z2s = sb("z2s%d" % c, [P, c1 - c0], U8)
-            nc.vector.quantize_mx(z2w[:].bitcast(FP8X4), z2s[:], zc[:])
-            for t in range(PLANES):
-                nc.tensor.matmul_mx(
-                    s_banks[t][:, c0:c1],
-                    lhsT=zw[:, P * t : P * (t + 1)].bitcast(FP8X4),
-                    lhsT_scale=zs[:, P * t : P * (t + 1)],
-                    rhs=z2w[:].bitcast(FP8X4),
-                    rhs_scale=z2s[:],
-                    start=True,
-                    stop=True,
-                )
-            for t in range(PLANES):
-                nc.scalar.activation(ex_win[t][:, c0:c1], s_banks[t][:, c0:c1], ACT.Exp, scale=0.03125)
-            for t in range(PLANES):
-                nc.scalar.activation(ex4[:, t, c0:c1], s_banks[t][:, c0:c1], ACT.Exp, scale=0.03125)
-
-        zb = sb("zb", [P, PLANES * S], BF16)
-        zb_view = zb[:].rearrange("p (u m t) -> p m t u", u=4, t=4)
-        ga_a_view = ga_a[:].rearrange("p t (m u) -> p m t u", u=4)
-        seconds = [sb("second%d" % c, [P, PLANES, c1 - c0], F32) for c, (c0, c1) in enumerate(HALVES)]
-        diffs = [sb("diff%d" % c, [P, PLANES, c1 - c0], F32) for c, (c0, c1) in enumerate(HALVES)]
+            nc.scalar.activation(sig[:, t, :], b_win[t][:].indirect(l_n4[:]), ACT.Sigmoid, scale=2.0)
         for t in range(PLANES):
-            for c, (c0, c1) in enumerate(HALVES):
-                nc.vector.tensor_copy(seconds[c][:, t, :], a_win[t][:].indirect(entries(l_n2, c0, c1)))
-            for c, (c0, c1) in enumerate(HALVES):
-                nc.vector.tensor_tensor(diffs[c][:, t, :], a_win[t][:].indirect(entries(l_n1, c0, c1)), seconds[c][:, t, :], ALU.subtract)
-        for c, (c0, c1) in enumerate(HALVES):
+            nc.scalar.activation(gb_tanh[:, t, :], sig[:, t, :], ACT.Identity, scale=g_cols[:, 4 + t : 5 + t], bias=g_cols[:, 8 + t : 9 + t])
+
+        probe = sb("probe", [P, 2], F32)
+        second = sb("second", [P, PLANES, S], F32)
+        diff = sb("diff", [P, PLANES, S], F32)
+        for t in range(PLANES + 1):
+            if t < PLANES:
+                nc.vector.tensor_copy(second[:, t, :], a_win[t][:].indirect(l_n2[:]))
+            if t > 0:
+                nc.vector.tensor_tensor(diff[:, t - 1, :], a_win[t - 1][:].indirect(l_n1[:]), second[:, t - 1, :], ALU.subtract)
+
+        def z_pair(h, tag):
+            zb = sb("zb%d" % h, [P, 2 * S], BF16, tag=tag)
             nc.vector.tensor_tensor(
-                zb_view[:, c0 // 4 : c1 // 4],
-                diffs[c][:].rearrange("p t (m u) -> p m t u", u=4),
-                ga_a_view[:, c0 // 4 : c1 // 4],
+                zb[:].rearrange("p (u m t) -> p m t u", u=2, t=4),
+                diff[:].rearrange("p t (m u) -> p m t u", u=4)[:, :, :, 2 * h : 2 * h + 2],
+                ga_a[:].rearrange("p t (m u) -> p m t u", u=4)[:, :, :, 2 * h : 2 * h + 2],
                 ALU.mult,
             )
+            return zb
 
         s_banks = [psum.tile([P, S], F32, name="s_bank%d" % t, tag="bankA%d" % t) for t in range(PLANES)]
-        ex_win = [sb("ex_win%d" % t, [P, S], F32) for t in range(PLANES)]
+        ex_win = a_win
         ex4 = sb("ex4", [P, PLANES, S], F32)
-        zw = sb("zw", [P, S], U32)
-        zs = sb("zs", [P, S], U8)
+        zw = [sb("zw%d" % h, [P, 2 * P], U32) for h in range(2)]
+        zs = [sb("zs%d" % h, [P, 2 * P], U8) for h in range(2)]
+        z2w = sb("z2w", [P, S], U32)
+        z2s = sb("z2s", [P, S], U8)
+
+        def scores(t):
+            nc.tensor.matmul_mx(
+                s_banks[t][:],
+                lhsT=zw[t // 2][:, P * (t % 2) : P * (t % 2 + 1)].bitcast(FP8X4),
+                lhsT_scale=zs[t // 2][:, P * (t % 2) : P * (t % 2 + 1)],
+                rhs=z2w[:].bitcast(FP8X4),
+                rhs_scale=z2s[:],
+                start=True,
+                stop=True,
+            )
+            nc.scalar.activation(ex_win[t][:, 0:S], s_banks[t][:], ACT.Exp, scale=0.03125)
+            nc.scalar.activation(ex4[:, t, :], s_banks[t][:], ACT.Exp, scale=0.03125)
+
+        nc.gpsimd.tensor_copy(probe[:, 0:1], diff[:, 3, S - 1 : S])
+        zb = z_pair(0, None)
+        third = sb("third", [P, PLANES, S], F32)
+        for t in range(PLANES):
+            nc.vector.tensor_tensor(third[:, t, :], b_win[t][:].indirect(l_n3[:]), b_plain[:, t, :], ALU.mult)
+            if t == 0:
+                nc.vector.quantize_mx(zw[0][:].bitcast(FP8X4), zs[0][:], zb[:])
+        z2b = [sb("z2b%d" % c, [P, PLANES * (c1 - c0)], BF16) for c, (c0, c1) in enumerate(HALVES)]
         for c, (c0, c1) in enumerate(HALVES):
-            prod = sb("third%d" % c, [P, PLANES, c1 - c0], F32, tag="tanh0" if c == 1 else None)
-            for t in range(PLANES):
-                nc.vector.tensor_tensor(prod[:, t, :], b_win[t][:].indirect(entries(l_n3, c0, c1)), gb_b[:, t, c0:c1], ALU.mult)
-                if c == 0 and t == 0:
-                    nc.vector.quantize_mx(zw[:].bitcast(FP8X4), zs[:], zb[:])
-                if c == 1 and t == 0:
-                    scores(0, zc)
-            zc = sb("z2b%d" % c, [P, PLANES * (c1 - c0)], BF16)
             nc.vector.tensor_tensor(
-                zc[:].rearrange("p (c i t) -> p c t i", i=4, t=4),
-                prod[:].rearrange("p t (c i) -> p c t i", i=4),
-                tanh4[c][:].rearrange("p t (c i) -> p c t i", i=4),
+                z2b[c][:].rearrange("p (c i t) -> p c t i", i=4, t=4),
+                third[:, :, c0:c1].rearrange("p t (c i) -> p c t i", i=4),
+                gb_tanh[:, :, c0:c1].rearrange("p t (c i) -> p c t i", i=4),
                 ALU.mult,
             )
-        scores(1, zc)
+        for c, (c0, c1) in enumerate(HALVES):
+            nc.vector.quantize_mx(z2w[:, c0:c1].bitcast(FP8X4), z2s[:, c0:c1], z2b[c][:])
+        scores(0)
+        scores(1)
+        zb = z_pair(1, "gb_tanh")
+        nc.vector.quantize_mx(zw[1][:].bitcast(FP8X4), zs[1][:], zb[:])
+        scores(2)
+        scores(3)
 
         yw = sb("yw", [P, S], U32)
         ys = sb("ys", [P, S], U8)
         out_rows = out_0.rearrange("(p t) v -> p t v", t=4)
         out_words = out_1[0].rearrange("p n t -> p (n t)").bitcast(I32)
 
-        def gathers(c):
-            c0, c1 = TAIL[c]
-            part = sb("part%d" % c, [P, PLANES, c1 - c0], F32, tag="inv0" if c == 2 else None)
-            den = sb("den%d" % c, [P, PLANES, c1 - c0], F32)
-            for t in range(PLANES):
-                nc.vector.tensor_tensor(part[:, t, :], ex_win[t][:].indirect(entries(l_n5, c0, c1)), ex4[:, t, c0:c1], ALU.add)
-            for t in range(PLANES):
-                nc.vector.tensor_tensor(den[:, t, :], ex_win[t][:].indirect(entries(l_n6, c0, c1)), part[:, t, :], ALU.add)
-            root = sb("root%d" % c, [P, PLANES, c1 - c0], F32)
-            inv = sb("inv%d" % c, [P, PLANES, c1 - c0], F32)
-            for t0, t1 in ((0, 2), (2, 4)) if c == 2 else ((0, 4),):
-                nc.scalar.activation(root[:, t0:t1, :], den[:, t0:t1, :], ACT.Abs_reciprocal_sqrt, scale=0.5)
-                nc.scalar.activation(inv[:, t0:t1, :], root[:, t0:t1, :], ACT.Square)
-            return inv
+        part = sb("part", [P, PLANES, S], F32)
+        den = sb("den", [P, PLANES, S], F32)
+        root = sb("root", [P, PLANES, S], F32)
+        inv = sb("inv", [P, PLANES, S], F32)
+        y = sb("y", [P, PLANES, S], F32)
+        pieces = [(0, 0, S), (1, 0, S), (2, 0, S), (3, 0, S // 2), (3, S // 2, S)]
 
-        def finish(c, inv):
-            c0, c1 = TAIL[c]
-            y = sb("y%d" % c, [P, PLANES, c1 - c0], F32)
-            nc.vector.tensor_tensor(y[:], ex4[:, :, c0:c1], inv[:], ALU.mult)
-            nc.sync.dma_start(out_rows[:, :, c0:c1], y[:])
+        def first_sum(t, c0, c1):
+            nc.vector.tensor_tensor(part[:, t, c0:c1], ex_win[t][:].indirect(entries(l_n5, c0, c1)), ex4[:, t, c0:c1], ALU.add)
+
+        def second_sum(t, c0, c1):
+            nc.vector.tensor_tensor(den[:, t, c0:c1], ex_win[t][:].indirect(entries(l_n6, c0, c1)), part[:, t, c0:c1], ALU.add)
+            nc.scalar.activation(root[:, t, c0:c1], den[:, t, c0:c1], ACT.Abs_reciprocal_sqrt, scale=0.5)
+            nc.scalar.activation(inv[:, t, c0:c1], root[:, t, c0:c1], ACT.Square)
+
+        def share(t, c0, c1):
+            nc.vector.tensor_tensor(y[:, t, c0:c1], ex4[:, t, c0:c1], inv[:, t, c0:c1], ALU.mult)
+            nc.sync.dma_start(out_rows[:, t, c0:c1], y[:, t, c0:c1])
+
+        def rounded(c, move):
+            c0, c1 = HALVES[c]
             yb = sb("yb%d" % c, [P, PLANES * (c1 - c0)], BF16)
-            move = nc.vector.tensor_copy if c == 2 else nc.scalar.copy
             move(
                 yb[:].rearrange("p (c i t) -> p c t i", i=4, t=4),
-                y[:].rearrange("p t (c i) -> p c t i", i=4),
+                y[:, :, c0:c1].rearrange("p t (c i) -> p c t i", i=4),
             )
             return yb
 
         def planes(c, yb):
-            c0, c1 = TAIL[c]
+            c0, c1 = HALVES[c]
             nc.vector.quantize_mx(yw[:, c0:c1].bitcast(FP8X4), ys[:, c0:c1], yb[:])
             nc.sync.dma_start(out_words[:, c0:c1], yw[:, c0:c1].bitcast(I32))
 
-        inv0 = gathers(0)
-        inv1 = gathers(1)
-        yb0 = finish(0, inv0)
-        inv2 = gathers(2)
-        yb1 = finish(1, inv1)
-        planes(0, yb0)
-        yb2 = finish(2, inv2)
+        for i in range(len(pieces) + 1):
+            if i < len(pieces):
+                first_sum(*pieces[i])
+            if i > 0:
+                second_sum(*pieces[i - 1])
+        nc.gpsimd.tensor_copy(probe[:, 1:2], den[:, 3, S - 1 : S])
+        for piece in pieces[:4]:
+            share(*piece)
+        yb0 = rounded(0, nc.scalar.copy)
+        share(*pieces[4])
+        yb1 = rounded(1, nc.vector.tensor_copy)
         planes(1, yb1)
-        planes(2, yb2)
+        planes(0, yb0)
         for q in range(4):
             queue = nc.scalar if q % 2 else nc.sync
             queue.dma_start(out_2[0, 4 * q : 4 * q + 4, :].bitcast(I32), ys[32 * q : 32 * q + 4, :].bitcast(I32))

@@ -20,7 +20,10 @@ P = 128
 T = 2048
 S = 512
 PLANES = 4
-HALVES = [(0, 256), (256, 512)]
+QUADRANTS = 4
+WINDOW = 2 * S
+HALVES = [(0, S // 2), (S // 2, S)]
+EXP_SCALE = 0.5 * 0.0625
 
 
 def tile_picked_kqwindcubeshare_none_po_kernel(
@@ -36,16 +39,22 @@ def tile_picked_kqwindcubeshare_none_po_kernel(
             return keep.tile(shape, dtype, name=name, tag=tag or name, align_bytes=64)
 
         def load_list(name, src):
-            t = keep.tile([P, S // 16], U16, name=name)
-            nc.sync.dma_start(t[:], src)
-            return t
+            lst = keep.tile([P, S // 16], U16, name=name)
+            nc.sync.dma_start(lst[:], src)
+            return lst
 
-        def load_scale_rows(dst, src, queue):
-            for q in range(4):
-                queue.dma_start(dst[32 * q : 32 * q + 4, :].bitcast(I32), src[0, 4 * q : 4 * q + 4, :].bitcast(I32))
+        def load_scale_rows(dst, src):
+            for quad in range(QUADRANTS):
+                nc.sync.dma_start(
+                    dst[32 * quad : 32 * quad + 4, :].bitcast(I32),
+                    src[0, 4 * quad : 4 * quad + 4, :].bitcast(I32),
+                )
 
-        def entries(lst, c0, c1):
-            return lst[:, c0 // 16 : c1 // 16]
+        def by_word(ap):
+            return ap.rearrange("p t (c i) -> p c t i", i=4)
+
+        def words_of(ap):
+            return ap.rearrange("p (c i t) -> p c t i", i=4, t=PLANES)
 
         xs = sb("xs", [P, T], U8)
         xw = sb("xw", [P, T], U32)
@@ -53,35 +62,33 @@ def tile_picked_kqwindcubeshare_none_po_kernel(
         w2s_raw = sb("w2s_raw", [P, S], U8)
         w1w_raw = sb("w1w_raw", [P, 2 * S], U8)
         w2w_raw = sb("w2w_raw", [P, 2 * S], U8)
-        g_rows = sb("g_rows", [P, P], F32)
+        gain_rows = sb("gain_rows", [P, P], F32)
         ident = sb("ident", [P, P], F32)
-        warm = sb("warm", [P, 2], F32)
 
         nc.gpsimd.memset(xs[:].bitcast(I32), 0)
         nc.vector.memset(w1s_raw[:].bitcast(I32), 0)
         nc.vector.memset(w2s_raw[:].bitcast(I32), 0)
-        nc.gpsimd.memset(g_rows[:], 0.0)
+        nc.gpsimd.memset(gain_rows[:], 0.0)
         make_identity(nc, ident[:])
-        nc.vector.memset(warm[:, 0:1], 0.0)
-        nc.scalar.activation(warm[:, 1:2], warm[:, 0:1], ACT.Sigmoid)
 
-        a_win = [sb("a_win%d" % t, [P, 2 * S], F32) for t in range(PLANES)]
-        b_win = [sb("b_win%d" % t, [P, 2 * S], F32) for t in range(PLANES)]
+        a_win = [sb("a_win%d" % t, [P, WINDOW], F32) for t in range(PLANES)]
+        b_win = [sb("b_win%d" % t, [P, WINDOW], F32) for t in range(PLANES)]
+        ex_win = [sb("ex_win%d" % t, [P, WINDOW], F32) for t in range(PLANES)]
 
         l_offs = load_list("l_offs", offs)
         l_two = load_list("l_two", two)
         nc.sync.dma_start(w1w_raw[:].bitcast(I32), w1_words[0].bitcast(I32))
-        load_scale_rows(xs, x_scales, nc.sync)
+        load_scale_rows(xs, x_scales)
         nc.sync.dma_start(xw[:].bitcast(I32), x_words[0].rearrange("p n t -> p (n t)").bitcast(I32))
-        load_scale_rows(w1s_raw, w1_scales, nc.sync)
+        load_scale_rows(w1s_raw, w1_scales)
         l_n2 = load_list("l_n2", n2)
         l_n1 = load_list("l_n1", n1)
         nc.sync.dma_start(w2w_raw[:].bitcast(I32), w2_words[0].bitcast(I32))
-        load_scale_rows(w2s_raw, w2_scales, nc.sync)
-        for i, g in enumerate((ga, gb)):
+        load_scale_rows(w2s_raw, w2_scales)
+        for i, gain in enumerate((ga, gb)):
             nc.sync.dma_start(
-                g_rows[4 * i : 4 * i + 4, :].rearrange("t (g q) -> t g q", q=8),
-                g.rearrange("(g t q) o -> t g (q o)", t=4, q=8),
+                gain_rows[PLANES * i : PLANES * (i + 1), :].rearrange("t (g q) -> t g q", q=8),
+                gain.rearrange("(g t q) o -> t g (q o)", t=PLANES, q=8),
             )
         l_n4 = load_list("l_n4", n4)
         l_n3 = load_list("l_n3", n3)
@@ -91,10 +98,10 @@ def tile_picked_kqwindcubeshare_none_po_kernel(
         def deal(name, raw_words, raw_scales):
             words = sb(name + "_words", [P, 2 * S], U8)
             scales = sb(name + "_scales", [P, S], U8)
-            for dst, src, w in ((words, raw_words, 4), (scales, raw_scales, 2)):
+            for dst, src, run in ((words, raw_words, 4), (scales, raw_scales, 2)):
                 nc.gpsimd.tensor_copy(
-                    dst[:].bitcast(I32).rearrange("p (t g w) -> p t g w", t=4, w=w),
-                    src[:].bitcast(I32).rearrange("p (g t w) -> p t g w", t=4, w=w),
+                    dst[:].bitcast(I32).rearrange("p (t g w) -> p t g w", t=PLANES, w=run),
+                    src[:].bitcast(I32).rearrange("p (g t w) -> p t g w", t=PLANES, w=run),
                 )
             return words, scales
 
@@ -109,23 +116,23 @@ def tile_picked_kqwindcubeshare_none_po_kernel(
         nc.vector.tensor_copy(xb_w[:], xw[:].indirect(l_two[:]))
         w2w, w2s = deal("w2", w2w_raw, w2s_raw)
 
-        g_bank = psum.tile([P, P], F32, name="g_bank", tag="bankB3")
-        nc.tensor.transpose(g_bank[:], g_rows[:], ident[:])
-        g_cols = sb("g_cols", [P, 12], F32)
-        nc.scalar.copy(g_cols[:, 0:4], g_bank[:, 0:4])
-        nc.scalar.activation(g_cols[:, 4:8], g_bank[:, 4:8], ACT.Copy, scale=2.0)
-        nc.scalar.activation(g_cols[:, 8:12], g_bank[:, 4:8], ACT.Copy, scale=-1.0)
+        gain_bank = psum.tile([P, P], F32, name="gain_bank", tag="bankB%d" % (PLANES - 1))
+        nc.tensor.transpose(gain_bank[:], gain_rows[:], ident[:])
+        gains = sb("gains", [P, 3 * PLANES], F32)
+        nc.scalar.copy(gains[:, 0:PLANES], gain_bank[:, 0:PLANES])
+        nc.scalar.activation(gains[:, PLANES : 2 * PLANES], gain_bank[:, PLANES : 2 * PLANES], ACT.Copy, scale=2.0)
+        nc.scalar.activation(gains[:, 2 * PLANES : 3 * PLANES], gain_bank[:, PLANES : 2 * PLANES], ACT.Copy, scale=-1.0)
 
-        def project(name, tag, ww, ws, xwords, xscales, windows):
+        def project(name, tag, w_words, w_scales, tok_words, tok_scales, windows):
             banks = []
             for t in range(PLANES):
                 bank = psum.tile([P, S], F32, name=name + "_bank%d" % t, tag=tag + "%d" % t)
                 nc.tensor.matmul_mx(
                     bank[:],
-                    lhsT=ww[:, 256 * t : 256 * (t + 1)].bitcast(FP4X4),
-                    lhsT_scale=ws[:, P * t : P * (t + 1)],
-                    rhs=xwords[:].bitcast(FP8X4),
-                    rhs_scale=xscales[:],
+                    lhsT=w_words[:, 2 * P * t : 2 * P * (t + 1)].bitcast(FP4X4),
+                    lhsT_scale=w_scales[:, P * t : P * (t + 1)],
+                    rhs=tok_words[:].bitcast(FP8X4),
+                    rhs_scale=tok_scales[:],
                     start=True,
                     stop=True,
                 )
@@ -141,82 +148,81 @@ def tile_picked_kqwindcubeshare_none_po_kernel(
         for t in range(PLANES):
             nc.sync.dma_start(b_plain[:, t, :], b_win[t][:, 0:S])
         for t in range(PLANES):
-            nc.scalar.activation(ga_a[:, t, :], a_banks[t][:], ACT.Copy, scale=g_cols[:, t : t + 1])
+            nc.scalar.activation(ga_a[:, t, :], a_banks[t][:], ACT.Copy, scale=gains[:, t : t + 1])
 
         sig = sb("sig", [P, PLANES, S], F32)
         gb_tanh = sb("gb_tanh", [P, PLANES, S], F32)
         for t in range(PLANES):
             nc.scalar.activation(sig[:, t, :], b_win[t][:].indirect(l_n4[:]), ACT.Sigmoid, scale=2.0)
         for t in range(PLANES):
-            nc.scalar.activation(gb_tanh[:, t, :], sig[:, t, :], ACT.Identity, scale=g_cols[:, 4 + t : 5 + t], bias=g_cols[:, 8 + t : 9 + t])
+            nc.scalar.activation(
+                gb_tanh[:, t, :], sig[:, t, :], ACT.Identity,
+                scale=gains[:, PLANES + t : PLANES + t + 1],
+                bias=gains[:, 2 * PLANES + t : 2 * PLANES + t + 1],
+            )
 
-        probe = sb("probe", [P, 2], F32)
-        second = sb("second", [P, PLANES, S], F32)
+        a_n2 = sb("a_n2", [P, PLANES, S], F32)
         diff = sb("diff", [P, PLANES, S], F32)
         for t in range(PLANES + 1):
             if t < PLANES:
-                nc.vector.tensor_copy(second[:, t, :], a_win[t][:].indirect(l_n2[:]))
+                nc.vector.tensor_copy(a_n2[:, t, :], a_win[t][:].indirect(l_n2[:]))
             if t > 0:
-                nc.vector.tensor_tensor(diff[:, t - 1, :], a_win[t - 1][:].indirect(l_n1[:]), second[:, t - 1, :], ALU.subtract)
+                nc.vector.tensor_tensor(diff[:, t - 1, :], a_win[t - 1][:].indirect(l_n1[:]), a_n2[:, t - 1, :], ALU.subtract)
 
         def z_pair(h, tag):
             zb = sb("zb%d" % h, [P, 2 * S], BF16, tag=tag)
             nc.vector.tensor_tensor(
-                zb[:].rearrange("p (u m t) -> p m t u", u=2, t=4),
-                diff[:].rearrange("p t (m u) -> p m t u", u=4)[:, :, :, 2 * h : 2 * h + 2],
-                ga_a[:].rearrange("p t (m u) -> p m t u", u=4)[:, :, :, 2 * h : 2 * h + 2],
+                zb[:].rearrange("p (u m t) -> p m t u", u=2, t=PLANES),
+                diff[:].rearrange("p t (m u) -> p m t u", u=PLANES)[:, :, :, 2 * h : 2 * h + 2],
+                ga_a[:].rearrange("p t (m u) -> p m t u", u=PLANES)[:, :, :, 2 * h : 2 * h + 2],
                 ALU.mult,
             )
             return zb
 
         s_banks = [psum.tile([P, S], F32, name="s_bank%d" % t, tag="bankA%d" % t) for t in range(PLANES)]
-        ex_win = a_win
-        ex4 = sb("ex4", [P, PLANES, S], F32)
+        ex_plain = sb("ex_plain", [P, PLANES, S], F32)
         zw = [sb("zw%d" % h, [P, 2 * P], U32) for h in range(2)]
         zs = [sb("zs%d" % h, [P, 2 * P], U8) for h in range(2)]
         z2w = sb("z2w", [P, S], U32)
         z2s = sb("z2s", [P, S], U8)
 
         def scores(t):
+            h, u = divmod(t, 2)
             nc.tensor.matmul_mx(
                 s_banks[t][:],
-                lhsT=zw[t // 2][:, P * (t % 2) : P * (t % 2 + 1)].bitcast(FP8X4),
-                lhsT_scale=zs[t // 2][:, P * (t % 2) : P * (t % 2 + 1)],
+                lhsT=zw[h][:, P * u : P * (u + 1)].bitcast(FP8X4),
+                lhsT_scale=zs[h][:, P * u : P * (u + 1)],
                 rhs=z2w[:].bitcast(FP8X4),
                 rhs_scale=z2s[:],
                 start=True,
                 stop=True,
             )
-            nc.scalar.activation(ex_win[t][:, 0:S], s_banks[t][:], ACT.Exp, scale=0.03125)
-            nc.scalar.activation(ex4[:, t, :], s_banks[t][:], ACT.Exp, scale=0.03125)
+            nc.scalar.activation(ex_win[t][:, 0:S], s_banks[t][:], ACT.Exp, scale=EXP_SCALE)
+            nc.scalar.activation(ex_plain[:, t, :], s_banks[t][:], ACT.Exp, scale=EXP_SCALE)
 
-        nc.gpsimd.tensor_copy(probe[:, 0:1], diff[:, 3, S - 1 : S])
-        zb = z_pair(0, None)
-        third = sb("third", [P, PLANES, S], F32)
+        zb_low = z_pair(0, None)
+        b_b3 = sb("b_b3", [P, PLANES, S], F32)
         for t in range(PLANES):
-            nc.vector.tensor_tensor(third[:, t, :], b_win[t][:].indirect(l_n3[:]), b_plain[:, t, :], ALU.mult)
+            nc.vector.tensor_tensor(b_b3[:, t, :], b_win[t][:].indirect(l_n3[:]), b_plain[:, t, :], ALU.mult)
             if t == 0:
-                nc.vector.quantize_mx(zw[0][:].bitcast(FP8X4), zs[0][:], zb[:])
+                nc.vector.quantize_mx(zw[0][:].bitcast(FP8X4), zs[0][:], zb_low[:])
         z2b = [sb("z2b%d" % c, [P, PLANES * (c1 - c0)], BF16) for c, (c0, c1) in enumerate(HALVES)]
         for c, (c0, c1) in enumerate(HALVES):
             nc.vector.tensor_tensor(
-                z2b[c][:].rearrange("p (c i t) -> p c t i", i=4, t=4),
-                third[:, :, c0:c1].rearrange("p t (c i) -> p c t i", i=4),
-                gb_tanh[:, :, c0:c1].rearrange("p t (c i) -> p c t i", i=4),
-                ALU.mult,
+                words_of(z2b[c][:]), by_word(b_b3[:, :, c0:c1]), by_word(gb_tanh[:, :, c0:c1]), ALU.mult
             )
         for c, (c0, c1) in enumerate(HALVES):
             nc.vector.quantize_mx(z2w[:, c0:c1].bitcast(FP8X4), z2s[:, c0:c1], z2b[c][:])
         scores(0)
         scores(1)
-        zb = z_pair(1, "gb_tanh")
-        nc.vector.quantize_mx(zw[1][:].bitcast(FP8X4), zs[1][:], zb[:])
+        zb_high = z_pair(1, "gb_tanh")
+        nc.vector.quantize_mx(zw[1][:].bitcast(FP8X4), zs[1][:], zb_high[:])
         scores(2)
         scores(3)
 
         yw = sb("yw", [P, S], U32)
         ys = sb("ys", [P, S], U8)
-        out_rows = out_0.rearrange("(p t) v -> p t v", t=4)
+        out_rows = out_0.rearrange("(p t) v -> p t v", t=PLANES)
         out_words = out_1[0].rearrange("p n t -> p (n t)").bitcast(I32)
 
         part = sb("part", [P, PLANES, S], F32)
@@ -224,30 +230,29 @@ def tile_picked_kqwindcubeshare_none_po_kernel(
         root = sb("root", [P, PLANES, S], F32)
         inv = sb("inv", [P, PLANES, S], F32)
         y = sb("y", [P, PLANES, S], F32)
-        pieces = [(0, 0, S), (1, 0, S), (2, 0, S), (3, 0, S // 2), (3, S // 2, S)]
+        pieces = [(t, 0, S) for t in range(PLANES - 1)] + [(PLANES - 1, c0, c1) for c0, c1 in HALVES]
 
         def first_sum(t, c0, c1):
-            nc.vector.tensor_tensor(part[:, t, c0:c1], ex_win[t][:].indirect(entries(l_n5, c0, c1)), ex4[:, t, c0:c1], ALU.add)
+            looked_up = ex_win[t][:].indirect(l_n5[:, c0 // 16 : c1 // 16])
+            nc.vector.tensor_tensor(part[:, t, c0:c1], looked_up, ex_plain[:, t, c0:c1], ALU.add)
 
         def second_sum(t, c0, c1):
-            nc.vector.tensor_tensor(den[:, t, c0:c1], ex_win[t][:].indirect(entries(l_n6, c0, c1)), part[:, t, c0:c1], ALU.add)
+            looked_up = ex_win[t][:].indirect(l_n6[:, c0 // 16 : c1 // 16])
+            nc.vector.tensor_tensor(den[:, t, c0:c1], looked_up, part[:, t, c0:c1], ALU.add)
             nc.scalar.activation(root[:, t, c0:c1], den[:, t, c0:c1], ACT.Abs_reciprocal_sqrt, scale=0.5)
             nc.scalar.activation(inv[:, t, c0:c1], root[:, t, c0:c1], ACT.Square)
 
         def share(t, c0, c1):
-            nc.vector.tensor_tensor(y[:, t, c0:c1], ex4[:, t, c0:c1], inv[:, t, c0:c1], ALU.mult)
+            nc.vector.tensor_tensor(y[:, t, c0:c1], ex_plain[:, t, c0:c1], inv[:, t, c0:c1], ALU.mult)
             nc.sync.dma_start(out_rows[:, t, c0:c1], y[:, t, c0:c1])
 
         def rounded(c, move):
             c0, c1 = HALVES[c]
             yb = sb("yb%d" % c, [P, PLANES * (c1 - c0)], BF16)
-            move(
-                yb[:].rearrange("p (c i t) -> p c t i", i=4, t=4),
-                y[:, :, c0:c1].rearrange("p t (c i) -> p c t i", i=4),
-            )
+            move(words_of(yb[:]), by_word(y[:, :, c0:c1]))
             return yb
 
-        def planes(c, yb):
+        def quantise_out(c, yb):
             c0, c1 = HALVES[c]
             nc.vector.quantize_mx(yw[:, c0:c1].bitcast(FP8X4), ys[:, c0:c1], yb[:])
             nc.sync.dma_start(out_words[:, c0:c1], yw[:, c0:c1].bitcast(I32))
@@ -257,14 +262,16 @@ def tile_picked_kqwindcubeshare_none_po_kernel(
                 first_sum(*pieces[i])
             if i > 0:
                 second_sum(*pieces[i - 1])
-        nc.gpsimd.tensor_copy(probe[:, 1:2], den[:, 3, S - 1 : S])
-        for piece in pieces[:4]:
+        for piece in pieces[:-1]:
             share(*piece)
-        yb0 = rounded(0, nc.scalar.copy)
-        share(*pieces[4])
-        yb1 = rounded(1, nc.vector.tensor_copy)
-        planes(1, yb1)
-        planes(0, yb0)
-        for q in range(4):
-            queue = nc.scalar if q % 2 else nc.sync
-            queue.dma_start(out_2[0, 4 * q : 4 * q + 4, :].bitcast(I32), ys[32 * q : 32 * q + 4, :].bitcast(I32))
+        yb_first = rounded(0, nc.scalar.copy)
+        share(*pieces[-1])
+        yb_second = rounded(1, nc.vector.tensor_copy)
+        quantise_out(1, yb_second)
+        quantise_out(0, yb_first)
+        for quad in range(QUADRANTS):
+            queue = nc.scalar if quad % 2 else nc.sync
+            queue.dma_start(
+                out_2[0, 4 * quad : 4 * quad + 4, :].bitcast(I32),
+                ys[32 * quad : 32 * quad + 4, :].bitcast(I32),
+            )

@@ -198,6 +198,8 @@ def tile_picked_kqwindcubeshare_none_po_kernel(
                 stop=True,
             )
             nc.scalar.activation(ex_win[t][:, 0:S], s_banks[t][:], ACT.Exp, scale=EXP_SCALE)
+
+        def ex_again(t):
             nc.scalar.activation(ex_plain[:, t, :], s_banks[t][:], ACT.Exp, scale=EXP_SCALE)
 
         zb_low = z_pair(0, None)
@@ -215,10 +217,13 @@ def tile_picked_kqwindcubeshare_none_po_kernel(
             nc.vector.quantize_mx(z2w[:, c0:c1].bitcast(FP8X4), z2s[:, c0:c1], z2b[c][:])
         scores(0)
         scores(1)
+        ex_again(0)
+        ex_again(1)
         zb_high = z_pair(1, "gb_tanh")
         nc.vector.quantize_mx(zw[1][:].bitcast(FP8X4), zs[1][:], zb_high[:])
-        scores(2)
-        scores(3)
+        for t in (2, 3):
+            scores(t)
+            ex_again(t)
 
         yw = sb("yw", [P, S], U32)
         ys = sb("ys", [P, S], U8)

from contextlib import ExitStack

import concourse.mybir as mybir
from concourse.masks import make_identity

FLOPS = 805306368

F32 = mybir.dt.float32
BF16 = mybir.dt.bfloat16
I32 = mybir.dt.int32
U32 = mybir.dt.uint32
U16 = mybir.dt.uint16
U8 = mybir.dt.uint8
FP8X4 = mybir.dt.float8_e4m3fn_x4
FP4X4 = mybir.dt.float4_e2m1fn_x4
ACT = mybir.ActivationFunctionType
ALU = mybir.AluOpType

P = 128
T = 2048
S = 512
PLANES = 4
QUADRANTS = 4
WINDOW = 2 * S
HALVES = [(0, S // 2), (S // 2, S)]
EXP_SCALE = 0.5 * 0.0625


def tile_picked_kqwindcubeshare_none_po_kernel(
    tc, x_words, x_scales, w1_words, w1_scales, w2_words, w2_scales, ga, gb,
    offs, two, n1, n2, n3, n4, n5, n6, out_0, out_1, out_2,
):
    nc = tc.nc
    with ExitStack() as ctx:
        keep = ctx.enter_context(tc.tile_pool(name="keep", bufs=1))
        psum = ctx.enter_context(tc.psum_pool(name="psum", bufs=1))

        def sb(name, shape, dtype, tag=None):
            return keep.tile(shape, dtype, name=name, tag=tag or name, align_bytes=64)

        def load_list(name, src):
            lst = keep.tile([P, S // 16], U16, name=name)
            nc.sync.dma_start(lst[:], src)
            return lst

        def load_scale_rows(dst, src):
            for quad in range(QUADRANTS):
                nc.sync.dma_start(
                    dst[32 * quad : 32 * quad + 4, :].bitcast(I32),
                    src[0, 4 * quad : 4 * quad + 4, :].bitcast(I32),
                )

        def by_word(ap):
            return ap.rearrange("p t (c i) -> p c t i", i=4)

        def words_of(ap):
            return ap.rearrange("p (c i t) -> p c t i", i=4, t=PLANES)

        xs = sb("xs", [P, T], U8)
        xw = sb("xw", [P, T], U32)
        w1s_raw = sb("w1s_raw", [P, S], U8)
        w2s_raw = sb("w2s_raw", [P, S], U8)
        w1w_raw = sb("w1w_raw", [P, 2 * S], U8)
        w2w_raw = sb("w2w_raw", [P, 2 * S], U8)
        gain_rows = sb("gain_rows", [P, P], F32)
        ident = sb("ident", [P, P], F32)

        nc.gpsimd.memset(xs[:].bitcast(I32), 0)
        nc.vector.memset(w1s_raw[:].bitcast(I32), 0)
        nc.vector.memset(w2s_raw[:].bitcast(I32), 0)
        nc.gpsimd.memset(gain_rows[:], 0.0)
        make_identity(nc, ident[:])

        a_win = [sb("a_win%d" % t, [P, WINDOW], F32) for t in range(PLANES)]
        b_win = [sb("b_win%d" % t, [P, WINDOW], F32) for t in range(PLANES)]
        ex_win = [sb("ex_win%d" % t, [P, WINDOW], F32) for t in range(PLANES)]

        l_offs = load_list("l_offs", offs)
        l_two = load_list("l_two", two)
        nc.sync.dma_start(w1w_raw[:].bitcast(I32), w1_words[0].bitcast(I32))
        load_scale_rows(xs, x_scales)
        nc.sync.dma_start(xw[:].bitcast(I32), x_words[0].rearrange("p n t -> p (n t)").bitcast(I32))
        load_scale_rows(w1s_raw, w1_scales)
        l_n2 = load_list("l_n2", n2)
        l_n1 = load_list("l_n1", n1)
        nc.sync.dma_start(w2w_raw[:].bitcast(I32), w2_words[0].bitcast(I32))
        load_scale_rows(w2s_raw, w2_scales)
        for i, gain in enumerate((ga, gb)):
            nc.sync.dma_start(
                gain_rows[PLANES * i : PLANES * (i + 1), :].rearrange("t (g q) -> t g q", q=8),
                gain.rearrange("(g t q) o -> t g (q o)", t=PLANES, q=8),
            )
        l_n4 = load_list("l_n4", n4)
        l_n3 = load_list("l_n3", n3)
        l_n5 = load_list("l_n5", n5)
        l_n6 = load_list("l_n6", n6)

        def deal(name, raw_words, raw_scales):
            words = sb(name + "_words", [P, 2 * S], U8)
            scales = sb(name + "_scales", [P, S], U8)
            for dst, src, run in ((words, raw_words, 4), (scales, raw_scales, 2)):
                nc.gpsimd.tensor_copy(
                    dst[:].bitcast(I32).rearrange("p (t g w) -> p t g w", t=PLANES, w=run),
                    src[:].bitcast(I32).rearrange("p (g t w) -> p t g w", t=PLANES, w=run),
                )
            return words, scales

        xa_s = sb("xa_s", [P, S], U8)
        xb_s = sb("xb_s", [P, S], U8)
        xa_w = sb("xa_w", [P, S], U32)
        xb_w = sb("xb_w", [P, S], U32)
        nc.vector.tensor_copy(xa_s[:], xs[:].indirect(l_offs[:]))
        nc.vector.tensor_copy(xb_s[:], xs[:].indirect(l_two[:]))
        w1w, w1s = deal("w1", w1w_raw, w1s_raw)
        nc.vector.tensor_copy(xa_w[:], xw[:].indirect(l_offs[:]))
        nc.vector.tensor_copy(xb_w[:], xw[:].indirect(l_two[:]))
        w2w, w2s = deal("w2", w2w_raw, w2s_raw)

        gain_bank = psum.tile([P, P], F32, name="gain_bank", tag="bankB%d" % (PLANES - 1))
        nc.tensor.transpose(gain_bank[:], gain_rows[:], ident[:])
        gains = sb("gains", [P, 3 * PLANES], F32)
        nc.scalar.copy(gains[:, 0:PLANES], gain_bank[:, 0:PLANES])
        nc.scalar.activation(gains[:, PLANES : 2 * PLANES], gain_bank[:, PLANES : 2 * PLANES], ACT.Copy, scale=2.0)
        nc.scalar.activation(gains[:, 2 * PLANES : 3 * PLANES], gain_bank[:, PLANES : 2 * PLANES], ACT.Copy, scale=-1.0)

        def project(name, tag, w_words, w_scales, tok_words, tok_scales, windows):
            banks = []
            for t in range(PLANES):
                bank = psum.tile([P, S], F32, name=name + "_bank%d" % t, tag=tag + "%d" % t)
                nc.tensor.matmul_mx(
                    bank[:],
                    lhsT=w_words[:, 2 * P * t : 2 * P * (t + 1)].bitcast(FP4X4),
                    lhsT_scale=w_scales[:, P * t : P * (t + 1)],
                    rhs=tok_words[:].bitcast(FP8X4),
                    rhs_scale=tok_scales[:],
                    start=True,
                    stop=True,
                )
                nc.scalar.copy(windows[t][:, 0:S], bank[:])
                banks.append(bank)
            return banks

        a_banks = project("a", "bankA", w1w, w1s, xa_w, xa_s, a_win)
        project("b", "bankB", w2w, w2s, xb_w, xb_s, b_win)

        ga_a = sb("ga_a", [P, PLANES, S], F32)
        b_plain = sb("b_plain", [P, PLANES, S], F32)
        for t in range(PLANES):
            nc.sync.dma_start(b_plain[:, t, :], b_win[t][:, 0:S])
        for t in range(PLANES):
            nc.scalar.activation(ga_a[:, t, :], a_banks[t][:], ACT.Copy, scale=gains[:, t : t + 1])

        sig = sb("sig", [P, PLANES, S], F32)
        gb_tanh = sb("gb_tanh", [P, PLANES, S], F32)
        for t in range(PLANES):
            nc.scalar.activation(sig[:, t, :], b_win[t][:].indirect(l_n4[:]), ACT.Sigmoid, scale=2.0)
        for t in range(PLANES):
            nc.scalar.activation(
                gb_tanh[:, t, :], sig[:, t, :], ACT.Identity,
                scale=gains[:, PLANES + t : PLANES + t + 1],
                bias=gains[:, 2 * PLANES + t : 2 * PLANES + t + 1],
            )

        a_n2 = sb("a_n2", [P, PLANES, S], F32)
        diff = sb("diff", [P, PLANES, S], F32)
        for t in range(PLANES + 1):
            if t < PLANES:
                nc.vector.tensor_copy(a_n2[:, t, :], a_win[t][:].indirect(l_n2[:]))
            if t > 0:
                nc.vector.tensor_tensor(diff[:, t - 1, :], a_win[t - 1][:].indirect(l_n1[:]), a_n2[:, t - 1, :], ALU.subtract)

        def z_pair(h, tag):
            zb = sb("zb%d" % h, [P, 2 * S], BF16, tag=tag)
            nc.vector.tensor_tensor(
                zb[:].rearrange("p (u m t) -> p m t u", u=2, t=PLANES),
                diff[:].rearrange("p t (m u) -> p m t u", u=PLANES)[:, :, :, 2 * h : 2 * h + 2],
                ga_a[:].rearrange("p t (m u) -> p m t u", u=PLANES)[:, :, :, 2 * h : 2 * h + 2],
                ALU.mult,
            )
            return zb

        s_banks = [psum.tile([P, S], F32, name="s_bank%d" % t, tag="bankA%d" % t) for t in range(PLANES)]
        ex_plain = sb("ex_plain", [P, PLANES, S], F32)
        zw = [sb("zw%d" % h, [P, 2 * P], U32) for h in range(2)]
        zs = [sb("zs%d" % h, [P, 2 * P], U8) for h in range(2)]
        z2w = sb("z2w", [P, S], U32)
        z2s = sb("z2s", [P, S], U8)

        def scores(t):
            h, u = divmod(t, 2)
            nc.tensor.matmul_mx(
                s_banks[t][:],
                lhsT=zw[h][:, P * u : P * (u + 1)].bitcast(FP8X4),
                lhsT_scale=zs[h][:, P * u : P * (u + 1)],
                rhs=z2w[:].bitcast(FP8X4),
                rhs_scale=z2s[:],
                start=True,
                stop=True,
            )
            nc.scalar.activation(ex_win[t][:, 0:S], s_banks[t][:], ACT.Exp, scale=EXP_SCALE)

        def ex_again(t):
            nc.scalar.activation(ex_plain[:, t, :], s_banks[t][:], ACT.Exp, scale=EXP_SCALE)

        zb_low = z_pair(0, None)
        b_b3 = sb("b_b3", [P, PLANES, S], F32)
        for t in range(PLANES):
            nc.vector.tensor_tensor(b_b3[:, t, :], b_win[t][:].indirect(l_n3[:]), b_plain[:, t, :], ALU.mult)
            if t == 0:
                nc.vector.quantize_mx(zw[0][:].bitcast(FP8X4), zs[0][:], zb_low[:])
        z2b = [sb("z2b%d" % c, [P, PLANES * (c1 - c0)], BF16) for c, (c0, c1) in enumerate(HALVES)]
        for c, (c0, c1) in enumerate(HALVES):
            nc.vector.tensor_tensor(
                words_of(z2b[c][:]), by_word(b_b3[:, :, c0:c1]), by_word(gb_tanh[:, :, c0:c1]), ALU.mult
            )
        for c, (c0, c1) in enumerate(HALVES):
            nc.vector.quantize_mx(z2w[:, c0:c1].bitcast(FP8X4), z2s[:, c0:c1], z2b[c][:])
        scores(0)
        scores(1)
        ex_again(0)
        ex_again(1)
        zb_high = z_pair(1, "gb_tanh")
        nc.vector.quantize_mx(zw[1][:].bitcast(FP8X4), zs[1][:], zb_high[:])
        for t in (2, 3):
            scores(t)
            ex_again(t)

        yw = sb("yw", [P, S], U32)
        ys = sb("ys", [P, S], U8)
        out_rows = out_0.rearrange("(p t) v -> p t v", t=PLANES)
        out_words = out_1[0].rearrange("p n t -> p (n t)").bitcast(I32)

        part = sb("part", [P, PLANES, S], F32)
        den = sb("den", [P, PLANES, S], F32)
        root = sb("root", [P, PLANES, S], F32)
        inv = sb("inv", [P, PLANES, S], F32)
        y = sb("y", [P, PLANES, S], F32)
        pieces = [(t, 0, S) for t in range(PLANES - 1)] + [(PLANES - 1, c0, c1) for c0, c1 in HALVES]

        def first_sum(t, c0, c1):
            looked_up = ex_win[t][:].indirect(l_n5[:, c0 // 16 : c1 // 16])
            nc.vector.tensor_tensor(part[:, t, c0:c1], looked_up, ex_plain[:, t, c0:c1], ALU.add)

        def second_sum(t, c0, c1):
            looked_up = ex_win[t][:].indirect(l_n6[:, c0 // 16 : c1 // 16])
            nc.vector.tensor_tensor(den[:, t, c0:c1], looked_up, part[:, t, c0:c1], ALU.add)
            nc.scalar.activation(root[:, t, c0:c1], den[:, t, c0:c1], ACT.Abs_reciprocal_sqrt, scale=0.5)
            nc.scalar.activation(inv[:, t, c0:c1], root[:, t, c0:c1], ACT.Square)

        def share(t, c0, c1):
            nc.vector.tensor_tensor(y[:, t, c0:c1], ex_plain[:, t, c0:c1], inv[:, t, c0:c1], ALU.mult)
            nc.sync.dma_start(out_rows[:, t, c0:c1], y[:, t, c0:c1])

        def rounded(c, move):
            c0, c1 = HALVES[c]
            yb = sb("yb%d" % c, [P, PLANES * (c1 - c0)], BF16)
            move(words_of(yb[:]), by_word(y[:, :, c0:c1]))
            return yb

        def quantise_out(c, yb):
            c0, c1 = HALVES[c]
            nc.vector.quantize_mx(yw[:, c0:c1].bitcast(FP8X4), ys[:, c0:c1], yb[:])
            nc.sync.dma_start(out_words[:, c0:c1], yw[:, c0:c1].bitcast(I32))

        for i in range(len(pieces) + 1):
            if i < len(pieces):
                first_sum(*pieces[i])
            if i > 0:
                second_sum(*pieces[i - 1])
        for piece in pieces[:-1]:
            share(*piece)
        yb_first = rounded(0, nc.scalar.copy)
        share(*pieces[-1])
        yb_second = rounded(1, nc.vector.tensor_copy)
        quantise_out(1, yb_second)
        quantise_out(0, yb_first)
        for quad in range(QUADRANTS):
            queue = nc.scalar if quad % 2 else nc.sync
            queue.dma_start(
                out_2[0, 4 * quad : 4 * quad + 4, :].bitcast(I32),
                ys[32 * quad : 32 * quad + 4, :].bitcast(I32),
            )
